import numpy as np, ml_dtypes
CORES = [16,32,48,64,80]
N = 5
TK = 256
def setup_inputs(rng):
    return {"c": rng.standard_normal((N, 128, 128), dtype=np.float32).astype(ml_dtypes.bfloat16), "x": rng.standard_normal((N, 128, TK), dtype=np.float32).astype(ml_dtypes.bfloat16)}
def setup_inputs_big(rng):
    d = setup_inputs(rng)
    for k in ("c", "x"): d[k] = (d[k].astype(np.float32) * 1024.0).astype(d[k].dtype)
    return d
def setup_inputs_small(rng):
    d = setup_inputs(rng)
    for k in ("c", "x"): d[k] = (d[k].astype(np.float32) * (1 / 1024.0)).astype(d[k].dtype)
    return d
def setup_inputs_apart(rng):
    d = setup_inputs(rng)
    f = (10.0 ** rng.permutation(np.linspace(-1.5, 1.5, N))).astype(np.float32).reshape(N, 1, 1)
    for k in ("c", "x"): d[k] = (d[k].astype(np.float32) * f).astype(d[k].dtype)
    return d
def reference(c, x):
    C, X = c.astype(np.float64), x.astype(np.float64)
    y = np.zeros((N, 128, TK))
    for r in range(N):
        for j in range(N):
            y[r] += C[(r - j) % N].T @ X[j]
    return {"y": y.astype(ml_dtypes.bfloat16 if x.dtype != np.float64 else np.float64)}

@@ -1,0 +1,73 @@
+from concourse.bass import DstId, RemoteDMATransfer
+
+N = 5
+KC = 128
+TK = 256
+W = KC + TK
+
+SCRATCH = {
+    "all": ("sbuf", [128, N * W], "bfloat16"),
+    "acc": ("psum", [128, TK], "float32"),
+    "out": ("sbuf", [128, TK], "bfloat16"),
+}
+SEMAPHORES = ["loaded", "sent", "mm", "cast", "stored"] + ["arr%d" % j for j in range(N)]
+
+
+def rank_program(g, core, T, topo):
+    r = T.rank_of(core)
+    if r is None:
+        return
+    n = len(T.cores)
+    buf = T.all
+
+    def slot(j):
+        return buf[:, j * W:(j + 1) * W]
+
+    def c_of(j):
+        return buf[:, j * W:j * W + KC]
+
+    def x_of(j):
+        return buf[:, j * W + KC:(j + 1) * W]
+
+    g.sync.dma_start(c_of(r), T.c[:]).then_inc(T.sem.loaded, 16)
+    g.scalar.dma_start(x_of(r), T.x[:]).then_inc(T.sem.loaded, 16)
+
+    peers = [T.cores[(r + d) % n] for d in range(1, n)]
+    mask = topo.mask(core, peers[0])
+    for p in peers:
+        assert topo.may_write(core, p)
+        mask &= topo.mask(core, p)
+    n_eng = bin(mask).count("1")
+    ids = []
+    for p in peers:
+        rid, pid, _ = topo.addr(p)
+        ids.append(DstId(rid=rid, pnc=pid))
+    g.wait_ge(T.sem.loaded, 32)
+    g.remote_dma_fused(
+        [RemoteDMATransfer(dst_ids=ids, dma_engine_mask=mask, remote_sem=T.sem["arr%d" % r],
+                           srcs=[slot(r)], dsts=[slot(r) for _ in peers], alu_op=0)],
+        local_sem=T.sem.sent)
+
+    have, done, plan = [], [], []
+    for d in range(n):
+        s = (r - d) % n
+        have.append(s)
+        ready = [j for j in range(n) if j not in done and j in have and (r - j) % n in have]
+        done += ready
+        plan.append((s, ready))
+    count = 0
+    for s, ready in plan:
+        if s == r:
+            g.tensor.wait_ge(T.sem.loaded, 32)
+        else:
+            g.tensor.wait_ge(T.sem["arr%d" % s], n_eng)
+        for j in ready:
+            g.tensor.matmul(T.acc[:], c_of((r - j) % n), x_of(j), count == 0, count == n - 1).then_inc(T.sem.mm, 1)
+            count += 1
+
+    g.vector.wait_ge(T.sem.mm, n)
+    g.vector.tensor_copy(T.out[:], T.acc[:]).then_inc(T.sem.cast, 1)
+    g.sync.wait_ge(T.sem.cast, 1)
+    g.sync.dma_start(T.y[:], T.out[:]).then_inc(T.sem.stored, 16)
+    g.sync.wait_ge(T.sem.stored, 16)
+    g.wait_ge(T.sem.sent, n_eng)

@@ -4,19 +4,36 @@ N = 5
 KC = 128
 TK = 256
 W = KC + TK
+BLOCKS = [(0, 64), (64, 128), (128, 192), (192, 256)]
 
 SCRATCH = {
+    "cst": ("dram", [128, KC], "bfloat16"),
+    "cl": ("dram", [128, KC], "bfloat16"),
     "all": ("sbuf", [128, N * W], "bfloat16"),
-    "acc": ("psum", [128, TK], "float32"),
     "out": ("sbuf", [128, TK], "bfloat16"),
 }
-SEMAPHORES = ["loaded", "sent", "mm", "cast", "stored"] + ["arr%d" % j for j in range(N)]
+for _b in range(len(BLOCKS)):
+    SCRATCH["acc%d" % _b] = ("psum", [128, 512], "float32")
+SEMAPHORES = (["staged", "loaded", "sent", "crel", "carr", "xarr", "cast", "stored"]
+              + ["arr%d" % j for j in range(N)] + ["mm%d" % b for b in range(len(BLOCKS))])
+
+
+def _bits(m):
+    return bin(m).count("1")
+
+
+def _relay(T, topo, q):
+    n = len(T.cores)
+    home, sender = T.cores[q], T.cores[(q + 1) % n]
+    for c in range(topo.CHIPS * topo.CORES_PER_CHIP):
+        if c in T.cores or topo.chip(c) != topo.chip(home) or topo.die(c) != topo.die(home):
+            continue
+        if topo.may_write(sender, c) and topo.may_write(c, home):
+            return c
+    return None
 
 
 def rank_program(g, core, T, topo):
-    r = T.rank_of(core)
-    if r is None:
-        return
     n = len(T.cores)
     buf = T.all
 
@@ -26,48 +43,77 @@ def rank_program(g, core, T, topo):
     def c_of(j):
         return buf[:, j * W:j * W + KC]
 
-    def x_of(j):
-        return buf[:, j * W + KC:(j + 1) * W]
+    def x_of(j, a, b):
+        return buf[:, j * W + KC + a:j * W + KC + b]
 
+    relays = [_relay(T, topo, q) for q in range(n)]
+
+    def relay_mask(q):
+        return topo.mask(relays[q], T.cores[q]) & topo.mask(relays[q], T.cores[(q + 1) % n])
+
+    r = T.rank_of(core)
+
+    if r is None:
+        if core not in relays:
+            return
+        q = relays.index(core)
+        s = (q + 1) % n
+        rid, pid, _ = topo.addr(T.cores[q])
+        g.wait_ge(T.sem.crel, _bits(topo.mask(T.cores[s], core)))
+        g.remote_dma(c_of(s), T.cl[:], T.sem.carr, T.sem.sent, pid, rid, relay_mask(q))
+        g.wait_ge(T.sem.sent, _bits(relay_mask(q)))
+        return
+
+    g.sync.dma_start(T.cst[:], T.c[:]).then_inc(T.sem.staged, 16)
+    g.scalar.dma_start(x_of(r, 0, TK), T.x[:]).then_inc(T.sem.loaded, 16)
     g.sync.dma_start(c_of(r), T.c[:]).then_inc(T.sem.loaded, 16)
-    g.scalar.dma_start(x_of(r), T.x[:]).then_inc(T.sem.loaded, 16)
 
     peers = [T.cores[(r + d) % n] for d in range(1, n)]
     mask = topo.mask(core, peers[0])
     for p in peers:
         assert topo.may_write(core, p)
         mask &= topo.mask(core, p)
-    n_eng = bin(mask).count("1")
+    n_eng = _bits(mask)
+    whole, last = peers[:-1], peers[-1]
     ids = []
-    for p in peers:
+    for p in whole:
         rid, pid, _ = topo.addr(p)
         ids.append(DstId(rid=rid, pnc=pid))
+    lrid, lpid, _ = topo.addr(last)
+    helper = relays[(r + n - 1) % n]
+    hrid, hpid, _ = topo.addr(helper)
+    hmask = topo.mask(core, helper)
+    g.wait_ge(T.sem.staged, 16)
+    g.remote_dma(T.cl[:], T.cst[:], T.sem.crel, T.sem.sent, hpid, hrid, hmask)
     g.wait_ge(T.sem.loaded, 32)
     g.remote_dma_fused(
         [RemoteDMATransfer(dst_ids=ids, dma_engine_mask=mask, remote_sem=T.sem["arr%d" % r],
-                           srcs=[slot(r)], dsts=[slot(r) for _ in peers], alu_op=0)],
+                           srcs=[slot(r)], dsts=[slot(r) for _ in whole], alu_op=0)],
         local_sem=T.sem.sent)
+    g.remote_dma(x_of(r, 0, TK), x_of(r, 0, TK), T.sem.xarr, T.sem.sent, lpid, lrid, mask)
 
-    have, done, plan = [], [], []
-    for d in range(n):
-        s = (r - d) % n
-        have.append(s)
-        ready = [j for j in range(n) if j not in done and j in have and (r - j) % n in have]
+    split = (r + 1) % n
+    full = [("arr%d" % ((r - d) % n), n_eng, [(r - d) % n], [(r - d) % n]) for d in range(1, n - 1)]
+    events = ([("loaded", 32, [r], [r])] + full[:2] + [("carr", _bits(relay_mask(r)), [split], [])]
+              + full[2:] + [("xarr", n_eng, [], [split])])
+    have_c, have_x, done = [], [], []
+    for sem, val, cs, xs in events:
+        have_c += cs
+        have_x += xs
+        ready = [j for j in range(n) if j not in done and j in have_x and (r - j) % n in have_c]
+        g.tensor.wait_ge(T.sem[sem], val)
+        for b, (lo, hi) in enumerate(BLOCKS):
+            for i, j in enumerate(ready):
+                k = len(done) + i
+                g.tensor.matmul(T["acc%d" % b][:, 0:hi - lo], c_of((r - j) % n), x_of(j, lo, hi),
+                                k == 0, k == n - 1).then_inc(T.sem["mm%d" % b], 1)
         done += ready
-        plan.append((s, ready))
-    count = 0
-    for s, ready in plan:
-        if s == r:
-            g.tensor.wait_ge(T.sem.loaded, 32)
-        else:
-            g.tensor.wait_ge(T.sem["arr%d" % s], n_eng)
-        for j in ready:
-            g.tensor.matmul(T.acc[:], c_of((r - j) % n), x_of(j), count == 0, count == n - 1).then_inc(T.sem.mm, 1)
-            count += 1
 
-    g.vector.wait_ge(T.sem.mm, n)
-    g.vector.tensor_copy(T.out[:], T.acc[:]).then_inc(T.sem.cast, 1)
-    g.sync.wait_ge(T.sem.cast, 1)
+    for b, (lo, hi) in enumerate(BLOCKS):
+        g.vector.wait_ge(T.sem["mm%d" % b], n)
+        g.vector.tensor_copy(T.out[:, lo:hi], T["acc%d" % b][:, 0:hi - lo]).then_inc(T.sem.cast, 1)
+
+    g.sync.wait_ge(T.sem.cast, len(BLOCKS))
     g.sync.dma_start(T.y[:], T.out[:]).then_inc(T.sem.stored, 16)
     g.sync.wait_ge(T.sem.stored, 16)
-    g.wait_ge(T.sem.sent, n_eng)
+    g.wait_ge(T.sem.sent, _bits(hmask) + 2 * n_eng)

from concourse.bass import DstId, RemoteDMATransfer

N = 5
KC = 128
TK = 256
W = KC + TK
BLOCKS = [(0, 64), (64, 128), (128, 192), (192, 256)]

SCRATCH = {
    "cst": ("dram", [128, KC], "bfloat16"),
    "cl": ("dram", [128, KC], "bfloat16"),
    "all": ("sbuf", [128, N * W], "bfloat16"),
    "out": ("sbuf", [128, TK], "bfloat16"),
}
for _b in range(len(BLOCKS)):
    SCRATCH["acc%d" % _b] = ("psum", [128, 512], "float32")
SEMAPHORES = (["staged", "loaded", "sent", "crel", "carr", "xarr", "cast", "stored"]
              + ["arr%d" % j for j in range(N)] + ["mm%d" % b for b in range(len(BLOCKS))])


def _bits(m):
    return bin(m).count("1")


def _relay(T, topo, q):
    n = len(T.cores)
    home, sender = T.cores[q], T.cores[(q + 1) % n]
    for c in range(topo.CHIPS * topo.CORES_PER_CHIP):
        if c in T.cores or topo.chip(c) != topo.chip(home) or topo.die(c) != topo.die(home):
            continue
        if topo.may_write(sender, c) and topo.may_write(c, home):
            return c
    return None


def rank_program(g, core, T, topo):
    n = len(T.cores)
    buf = T.all

    def slot(j):
        return buf[:, j * W:(j + 1) * W]

    def c_of(j):
        return buf[:, j * W:j * W + KC]

    def x_of(j, a, b):
        return buf[:, j * W + KC + a:j * W + KC + b]

    relays = [_relay(T, topo, q) for q in range(n)]

    def relay_mask(q):
        return topo.mask(relays[q], T.cores[q]) & topo.mask(relays[q], T.cores[(q + 1) % n])

    r = T.rank_of(core)

    if r is None:
        if core not in relays:
            return
        q = relays.index(core)
        s = (q + 1) % n
        rid, pid, _ = topo.addr(T.cores[q])
        g.wait_ge(T.sem.crel, _bits(topo.mask(T.cores[s], core)))
        g.remote_dma(c_of(s), T.cl[:], T.sem.carr, T.sem.sent, pid, rid, relay_mask(q))
        g.wait_ge(T.sem.sent, _bits(relay_mask(q)))
        return

    g.sync.dma_start(T.cst[:], T.c[:]).then_inc(T.sem.staged, 16)
    g.scalar.dma_start(x_of(r, 0, TK), T.x[:]).then_inc(T.sem.loaded, 16)
    g.sync.dma_start(c_of(r), T.c[:]).then_inc(T.sem.loaded, 16)

    peers = [T.cores[(r + d) % n] for d in range(1, n)]
    mask = topo.mask(core, peers[0])
    for p in peers:
        assert topo.may_write(core, p)
        mask &= topo.mask(core, p)
    n_eng = _bits(mask)
    whole, last = peers[:-1], peers[-1]
    ids = []
    for p in whole:
        rid, pid, _ = topo.addr(p)
        ids.append(DstId(rid=rid, pnc=pid))
    lrid, lpid, _ = topo.addr(last)
    helper = relays[(r + n - 1) % n]
    hrid, hpid, _ = topo.addr(helper)
    hmask = topo.mask(core, helper)
    g.wait_ge(T.sem.staged, 16)
    g.remote_dma(T.cl[:], T.cst[:], T.sem.crel, T.sem.sent, hpid, hrid, hmask)
    g.wait_ge(T.sem.loaded, 32)
    g.remote_dma_fused(
        [RemoteDMATransfer(dst_ids=ids, dma_engine_mask=mask, remote_sem=T.sem["arr%d" % r],
                           srcs=[slot(r)], dsts=[slot(r) for _ in whole], alu_op=0)],
        local_sem=T.sem.sent)
    g.remote_dma(x_of(r, 0, TK), x_of(r, 0, TK), T.sem.xarr, T.sem.sent, lpid, lrid, mask)

    split = (r + 1) % n
    full = [("arr%d" % ((r - d) % n), n_eng, [(r - d) % n], [(r - d) % n]) for d in range(1, n - 1)]
    events = ([("loaded", 32, [r], [r])] + full[:2] + [("carr", _bits(relay_mask(r)), [split], [])]
              + full[2:] + [("xarr", n_eng, [], [split])])
    have_c, have_x, done = [], [], []
    for sem, val, cs, xs in events:
        have_c += cs
        have_x += xs
        ready = [j for j in range(n) if j not in done and j in have_x and (r - j) % n in have_c]
        g.tensor.wait_ge(T.sem[sem], val)
        for b, (lo, hi) in enumerate(BLOCKS):
            for i, j in enumerate(ready):
                k = len(done) + i
                g.tensor.matmul(T["acc%d" % b][:, 0:hi - lo], c_of((r - j) % n), x_of(j, lo, hi),
                                k == 0, k == n - 1).then_inc(T.sem["mm%d" % b], 1)
        done += ready

    for b, (lo, hi) in enumerate(BLOCKS):
        g.vector.wait_ge(T.sem["mm%d" % b], n)
        g.vector.tensor_copy(T.out[:, lo:hi], T["acc%d" % b][:, 0:hi - lo]).then_inc(T.sem.cast, 1)

    g.sync.wait_ge(T.sem.cast, len(BLOCKS))
    g.sync.dma_start(T.y[:], T.out[:]).then_inc(T.sem.stored, 16)
    g.sync.wait_ge(T.sem.stored, 16)
    g.wait_ge(T.sem.sent, _bits(hmask) + 2 * n_eng)
